import numpy as np
import ml_dtypes


def mxq(x, axis, fmt="e4m3"):
    dtype, down = {"e4m3": (ml_dtypes.float8_e4m3fn, 7), "e5m2": (ml_dtypes.float8_e5m2, 14)}[fmt]
    v = np.moveaxis(np.asarray(x, np.float32).astype(ml_dtypes.bfloat16).astype(np.float64), axis, -1)
    blocks = v.reshape(v.shape[:-1] + (-1, 32))
    amax = np.abs(blocks).max(-1, keepdims=True)
    byte = np.maximum(np.where(amax > 0, np.frexp(amax)[1] - 1 + 127, 0) - down, 1)
    scale = np.exp2(byte - 127.0)
    codes = (blocks / scale).astype(np.float32).astype(dtype).astype(np.float64)
    return np.moveaxis((codes * scale).reshape(v.shape), -1, axis)


WIDE = False


def mx_kscale(k):
    if not WIDE:
        return np.ones(k)
    levels = np.array([10, -10, 5, -5, 0])
    if k % 512:
        return np.exp2(np.random.permutation(np.resize(levels, k // 32))).repeat(32)
    a = np.empty((k // 512, 16))
    for p in range(k // 512):
        a[p, :8] = np.random.permutation(np.resize(levels, 8))
        for g in range(8):
            far = levels[np.abs(levels - a[p, g]) >= 10]
            a[p, g + 8] = far[np.random.randint(len(far))]
    return np.exp2(a.ravel()).repeat(32)


def f64(x):
    return np.asarray(x).astype(np.float64)


def striped(idx):
    return np.tile(np.asarray(idx).reshape(-1, 16).T, (8, 1)).astype(np.uint16)


def unstriped(offs):
    return offs[:16].T.reshape(-1).astype(np.int64)


E2M1 = np.array([0.0, 0.5, 1.0, 1.5, 2.0, 3.0, 4.0, 6.0, -0.0, -0.5, -1.0, -1.5, -2.0, -3.0, -4.0, -6.0])


def pack_weight(w, fmt):
    k, n = w.shape
    w = f64(np.asarray(w, np.float32).astype(ml_dtypes.bfloat16)).reshape(k // 32, 32, n)
    amax = np.abs(w).max(1)
    if fmt == "e4m3":
        byte = np.frexp(amax)[1] - 1 + 127 - 7
    else:
        mant, ex = np.frexp(amax / 6.0)
        byte = np.where(mant > 0.5, ex, ex - 1) + 127
    byte = np.clip(np.where(amax > 0, byte, 1), 1, 254)
    scaled = (w * np.exp2(127.0 - byte)[:, None, :]).reshape(k, n).astype(np.float32)
    by_word = np.ascontiguousarray(scaled.reshape(k // 512, 128, 4, n).transpose(0, 1, 3, 2))
    if fmt == "e4m3":
        words = by_word.astype(ml_dtypes.float8_e4m3fn).view(np.uint8)
    else:
        c = by_word.astype(ml_dtypes.float4_e2m1fn).view(np.uint8) & 0xF
        words = (c[..., 0::2] | (c[..., 1::2] << 4)).reshape(k // 512, 128, 2 * n)
    return np.ascontiguousarray(words), np.ascontiguousarray(byte.astype(np.uint8).reshape(k // 512, 16, n))


def unpack_weight(words, scales, fmt):
    g, _, n = scales.shape
    words = np.ascontiguousarray(words).reshape(g, 128, n, -1)
    if fmt == "e4m3":
        vals = words.view(ml_dtypes.float8_e4m3fn).astype(np.float64)
    else:
        nib = np.empty((g, 128, n, 4), np.uint8)
        nib[..., 0::2] = words & 0xF
        nib[..., 1::2] = words >> 4
        vals = E2M1[nib]
    vals = vals * np.repeat(np.exp2(scales.astype(np.float64) - 127.0), 8, axis=1)[..., None]
    return vals.transpose(0, 1, 3, 2).reshape(g * 512, n)


def softplus(v):
    return np.log(1.0 + np.exp(v))


def sigmoid(v):
    return 1.0 / (1.0 + np.exp(-v))


D, K, R, T, I, Q, G = 512, 512, 512, 2048, 512, 128, 32


def setup_inputs():
    n = np.random.standard_normal
    idx = np.random.permutation(T)[:I]
    fd = mx_kscale(D)
    fk = mx_kscale(K)
    fr = mx_kscale(R)
    keysp = pack_weight(n((D, T)) / fd[:, None], "e4m3")
    tabp = pack_weight(n((K, T)) / fk[:, None], "e4m3")
    return {
        "query": (n((D, Q)) * 0.9 / np.sqrt(D) * fd[:, None]).astype(np.float32),
        "keys_words": keysp[0],
        "keys_scales": keysp[1],
        "th": (np.random.uniform(-0.3, 0.6, (Q, 1))).astype(np.float32),
        "reserve": (np.random.uniform(50.0, 200.0, (Q, 1))).astype(np.float32),
        "tab_words": tabp[0],
        "tab_scales": tabp[1],
        "w1": (n((K, R)) * 1 / np.sqrt(K) * fk[:, None]).astype(np.float32),
        "share": (np.random.uniform(0.4, 1.0, (R, 1))).astype(np.float32),
        "gout": (n((R, Q)) * 1 / np.sqrt(R) * fr[:, None]).astype(np.float32),
        "hsc": (np.random.uniform(0.7, 1.4, (R, 1)) / fr[:, None]).astype(np.float32),
        "old": (0.5 * n((Q, T))).astype(np.float32),
        "offs": striped(idx),
    }


def reference(query, keys_words, keys_scales, th, reserve, tab_words, tab_scales, w1, share, gout, hsc, old, offs):
    idx = unstriped(offs)
    keysu = unpack_weight(keys_words, keys_scales, "e4m3")
    tabu = unpack_weight(tab_words, tab_scales, "e4m3")
    queryq = mxq(f64(query), 0, "e4m3")
    keysidxg = keysu[:, idx]
    a = queryq.T @ keysidxg
    p = softplus(a - f64(th))
    z = np.sum(p, axis=1, keepdims=True) + f64(reserve)
    w1q = mxq(f64(w1), 0, "e4m3")
    tabidxg = tabu[:, idx]
    zh = w1q.T @ tabidxg
    mz = zh.reshape(R, G, I // G).mean(axis=2)
    mzr = np.repeat(mz, I // G, axis=1)
    hv = np.tanh(zh - mzr * f64(share))
    hs1 = hv * f64(hsc)
    goutq = mxq(f64(gout), 0, "e4m3")
    hs1q = mxq(hs1, 0, "e4m3")
    c0 = goutq.T @ hs1q
    dz = np.sum(c0 * p / np.square(z) * (-1.0), axis=1, keepdims=True)
    dp = c0 / z + dz
    da = dp * sigmoid(a - f64(th))
    gs = da * 512.0
    gf = np.zeros((Q, T))
    gf[:, idx] = gs
    y = f64(old) + gf
    return y

@@ -1,0 +1,204 @@
+from contextlib import ExitStack
+
+import concourse.mybir as mybir
+
+F32 = mybir.dt.float32
+BF16 = mybir.dt.bfloat16
+I32 = mybir.dt.int32
+U32 = mybir.dt.uint32
+U16 = mybir.dt.uint16
+U8 = mybir.dt.uint8
+FP8X4 = mybir.dt.float8_e4m3fn_x4
+ALU = mybir.AluOpType
+ACT = mybir.ActivationFunctionType
+AX = mybir.AxisListType
+
+P = 128
+PACK = 4
+POOL = 2048
+SLOTS = 512
+ROWS = 128
+HIDDEN = 512
+PAGE = 16
+CHUNK = 128
+CHUNKS = SLOTS // CHUNK
+PAGES = CHUNK // PAGE
+STORE = 512
+
+FLOPS = 2 * 512 * SLOTS * (ROWS + HIDDEN + ROWS)
+
+
+def tile_attend_blrcentred_capped_kernel(tc, query, keys_words, keys_scales, th, reserve, tab_words, tab_scales,
+                                          w1, share, gout, hsc, old, offs, out):
+    nc = tc.nc
+    with ExitStack() as ctx:
+        sb = ctx.enter_context(tc.tile_pool(name="sb", bufs=1))
+        ps = ctx.enter_context(tc.psum_pool(name="ps", bufs=1))
+
+        def sbuf(name, shape, dtype, tag=None):
+            return sb.tile(shape, dtype, name=name, tag=tag or name, align_bytes=64)
+
+        def load_scale_rows(queue, plane, scales):
+            for j in range(PACK):
+                queue.dma_start(out=plane[j:P:32, :].bitcast(I32), in_=scales[0, j:16:PACK, :].bitcast(I32))
+
+        def load_words(pool_words, words):
+            nc.sync.dma_start(out=pool_words[:], in_=words[0].rearrange("p n t -> p (n t)").bitcast(I32))
+
+        def quantize(codes, scales, grouped):
+            nc.vector.quantize_mx(out=codes.bitcast(FP8X4), scales=scales, in_=grouped)
+
+        def product(acc, lhs_codes, lhs_scales, rhs_codes, rhs_scales):
+            nc.tensor.matmul_mx(out=acc, lhsT=lhs_codes.bitcast(FP8X4), lhsT_scale=lhs_scales,
+                                rhs=rhs_codes.bitcast(FP8X4), rhs_scale=rhs_scales, start=True, stop=True)
+
+        offsets = sbuf("offsets", [P, SLOTS // 16], U16)
+        tab_plane = sbuf("tab_plane", [P, POOL], U8)
+        keys_plane = sbuf("keys_plane", [P, POOL], U8)
+        tab_pool = sbuf("tab_pool", [P, POOL], I32)
+        placed = sbuf("placed", [P, POOL], F32)
+        w_raw = sbuf("w_raw", [P, PACK, HIDDEN], F32)
+        q_raw = sbuf("q_raw", [P, PACK, ROWS], F32)
+        share_sb = sbuf("share_sb", [P, PACK], F32)
+        hsc_sb = sbuf("hsc_sb", [P, PACK], F32)
+        th_sb = sbuf("th_sb", [P, 1], F32)
+        reserve_sb = sbuf("reserve_sb", [P, 1], F32)
+
+        nc.vector.memset(tab_plane[:].bitcast(I32), 0)
+        nc.vector.memset(keys_plane[:].bitcast(I32), 0)
+        nc.vector.memset(placed[:], 0.0)
+
+        nc.sync.dma_start(offsets[:], offs)
+        nc.sync.dma_start(out=w_raw[:], in_=w1.rearrange("(p j) c -> p j c", j=PACK))
+        load_words(tab_pool, tab_words)
+        nc.sync.dma_start(out=q_raw[:], in_=query.rearrange("(p j) q -> p j q", j=PACK))
+        load_scale_rows(nc.scalar, tab_plane, tab_scales)
+        load_scale_rows(nc.gpsimd, keys_plane, keys_scales)
+        nc.gpsimd.dma_start(out=share_sb[:], in_=share.rearrange("(p t) o -> p (t o)", t=PACK))
+        nc.gpsimd.dma_start(out=th_sb[:], in_=th)
+        nc.gpsimd.dma_start(out=hsc_sb[:], in_=hsc.rearrange("(p t) o -> p (t o)", t=PACK))
+        nc.gpsimd.dma_start(out=reserve_sb[:], in_=reserve)
+
+        tab_scale = sbuf("tab_scale", [P, SLOTS], U8)
+        nc.vector.tensor_copy(tab_scale[:], tab_plane[:].indirect(offsets[:]))
+
+        w_grouped = sbuf("w_grouped", [P, PACK, P, PACK], BF16)
+        w_dst = w_grouped[:].rearrange("p t m j -> p m j t")
+        w_src = w_raw[:].rearrange("p j (m t) -> p m j t", t=PACK)
+        nc.scalar.copy(w_dst[:, 0:80], w_src[:, 0:80])
+        nc.vector.tensor_copy(w_dst[:, 80:128], w_src[:, 80:128])
+        keys_pool = sbuf("keys_pool", [P, POOL], I32, tag="w_raw")
+        load_words(keys_pool, keys_words)
+        keys_scale = sbuf("keys_scale", [P, SLOTS], U8)
+        nc.vector.tensor_copy(keys_scale[:], keys_plane[:].indirect(offsets[:]))
+        w_codes = sbuf("w_codes", [P, HIDDEN], U32)
+        w_scale = sbuf("w_scale", [P, HIDDEN], U8)
+        quantize(w_codes[:], w_scale[:], w_grouped[:].rearrange("p t m j -> p (t m j)"))
+
+        share_mean = sbuf("share_mean", [P, PACK], F32)
+        half_th = sbuf("half_th", [P, 1], F32)
+
+        tab_codes = sbuf("tab_codes", [P, SLOTS], U32)
+        for h in range(2):
+            nc.vector.tensor_copy(tab_codes[:, 256 * h:256 * (h + 1)],
+                                  tab_pool[:].bitcast(U32).indirect(offsets[:, 16 * h:16 * (h + 1)]))
+        old_sb = sbuf("old_sb", [P, POOL], F32, tag="tab_pool")
+        nc.vector.tensor_scalar(share_mean[:], share_sb[:], 1.0 / PAGE, None, ALU.mult)
+
+        def group_rows(raw, name):
+            grouped = sbuf(name, [P, ROWS, PACK], BF16)
+            nc.scalar.copy(grouped[:].rearrange("p (c i) j -> p c j i", i=4), raw[:].rearrange("p j (c i) -> p c j i", i=4))
+            return grouped
+
+        def layer(c):
+            cols = slice(c * CHUNK, (c + 1) * CHUNK)
+            zh = ps.tile([P, PACK, CHUNK], F32, name=f"zh{c}")
+            for t in range(PACK):
+                feats = slice(t * P, (t + 1) * P)
+                product(zh[:, t, :], w_codes[:, feats], w_scale[:, feats], tab_codes[:, cols], tab_scale[:, cols])
+            sums = sbuf(f"sums{c}", [P, PAGES, PACK], F32)
+            nc.vector.tensor_reduce(sums[:], zh[:].rearrange("p t (g j) -> p g t j", j=PAGE), AX.X, ALU.add)
+            shift = sbuf(f"shift{c}", [P, PAGES, PACK], F32)
+            nc.vector.tensor_tensor(shift[:], sums[:], share_mean[:].unsqueeze(1).to_broadcast([P, PAGES, PACK]), ALU.mult)
+            centred = sbuf(f"centred{c}", [P, PAGES, PAGE, PACK], F32)
+            nc.vector.tensor_tensor(centred[:], zh[:].rearrange("p t (g j) -> p g j t", j=PAGE),
+                                    shift[:].unsqueeze(2).to_broadcast([P, PAGES, PAGE, PACK]), ALU.subtract)
+            hv = sbuf(f"hv{c}", [P, CHUNK, PACK], F32)
+            nc.scalar.activation(hv[:].rearrange("p i t -> p (i t)"), centred[:].rearrange("p g j t -> p (g j t)"), ACT.Tanh)
+            return hv
+
+        hvs = [layer(0), layer(1)]
+
+        q_grouped = group_rows(q_raw, "q_grouped")
+        g_raw = sbuf("g_raw", [P, PACK, ROWS], F32, tag="q_raw")
+        nc.sync.dma_start(out=g_raw[:], in_=gout.rearrange("(p j) q -> p j q", j=PACK))
+        nc.sync.dma_start(out=old_sb[:], in_=old)
+        q_codes = sbuf("q_codes", [P, ROWS], U32)
+        q_scale = sbuf("q_scale", [P, ROWS], U8)
+        quantize(q_codes[:], q_scale[:], q_grouped[:].rearrange("p q j -> p (q j)"))
+        keys_codes = sbuf("keys_codes", [P, SLOTS], U32)
+        nc.vector.tensor_copy(keys_codes[:], keys_pool[:].bitcast(U32).indirect(offsets[:]))
+        nc.vector.tensor_scalar(half_th[:], th_sb[:], -0.5, None, ALU.mult)
+        score = ps.tile([P, SLOTS], F32, name="score")
+        product(score[:], q_codes[:], q_scale[:], keys_codes[:], keys_scale[:])
+        tanh_half = sbuf("tanh_half", [P, SLOTS], F32)
+        nc.scalar.activation(tanh_half[:], score[:], ACT.Tanh, bias=half_th[:], scale=0.5)
+        relu_half = sbuf("relu_half", [P, SLOTS], F32)
+        relu_sum = sbuf("relu_sum", [P, 1], F32)
+        nc.scalar.activation(relu_half[:], score[:], ACT.Relu, bias=half_th[:], scale=0.5, accum_out=relu_sum[:])
+        tanh_abs = sbuf("tanh_abs", [P, SLOTS], F32)
+        nc.scalar.activation(tanh_abs[:], tanh_half[:], ACT.Abs)
+
+        hvs = hvs + [layer(2), layer(3)]
+
+        g_grouped = group_rows(g_raw, "g_grouped")
+        g_codes = sbuf("g_codes", [P, ROWS], U32)
+        g_scale = sbuf("g_scale", [P, ROWS], U8)
+        quantize(g_codes[:], g_scale[:], g_grouped[:].rearrange("p q j -> p (q j)"))
+        z_part = sbuf("z_part", [P, 1], F32)
+        nc.vector.scalar_tensor_tensor(z_part[:], relu_sum[:], 2.0, reserve_sb[:], ALU.mult, ALU.add)
+
+        log_sig = sbuf("log_sig", [P, SLOTS], F32)
+        log_sum = sbuf("log_sum", [P, 1], F32)
+        nc.scalar.activation(log_sig[:], tanh_abs[:], ACT.Ln, bias=0.5, scale=0.5, accum_out=log_sum[:])
+        twice_sig = sbuf("twice_sig", [P, SLOTS], F32)
+        nc.scalar.activation(twice_sig[:], tanh_half[:], ACT.Identity, bias=1.0)
+
+        c0 = ps.tile([P, SLOTS], F32, name="c0")
+        hs_tiles = []
+        for c in range(CHUNKS):
+            hs = sbuf(f"hs{c}", [P, CHUNK, PACK], BF16)
+            nc.vector.tensor_tensor(hs[:], hvs[c][:], hsc_sb[:].unsqueeze(1).to_broadcast([P, CHUNK, PACK]), ALU.mult)
+            hs_tiles.append(hs)
+            if c >= 1:
+                finish = [c - 1] if c < CHUNKS - 1 else [c - 1, c]
+                for d in finish:
+                    hs_codes = sbuf(f"hs_codes{d}", [P, CHUNK], U32)
+                    hs_scale = sbuf(f"hs_scale{d}", [P, CHUNK], U8)
+                    quantize(hs_codes[:], hs_scale[:], hs_tiles[d][:].rearrange("p i t -> p (i t)"))
+                    product(c0[:, d * CHUNK:(d + 1) * CHUNK], g_codes[:], g_scale[:], hs_codes[:], hs_scale[:])
+
+        z = sbuf("z", [P, 1], F32)
+        nc.vector.tensor_tensor(z[:], z_part[:], log_sum[:], ALU.subtract)
+        soft = sbuf("soft", [P, SLOTS], F32)
+        nc.vector.scalar_tensor_tensor(soft[:], relu_half[:], 2.0, log_sig[:], ALU.mult, ALU.subtract)
+        z_inv = sbuf("z_inv", [P, 1], F32)
+        nc.vector.reciprocal(z_inv[:], z[:])
+        dz_factor = sbuf("dz_factor", [P, 1], F32)
+        nc.vector.tensor_scalar(dz_factor[:], z_inv[:], z_inv[:], -256.0, ALU.mult, ALU.mult)
+        dp_scale = sbuf("dp_scale", [P, 1], F32)
+        nc.vector.tensor_scalar(dp_scale[:], z_inv[:], 256.0, None, ALU.mult)
+        dz_terms = sbuf("dz_terms", [P, SLOTS], F32)
+        dz = sbuf("dz", [P, 1], F32)
+        nc.vector.scalar_tensor_tensor(dz_terms[:], c0[:], dz_factor[:], soft[:], ALU.mult, ALU.mult, accum_out=dz[:])
+
+        dp = sbuf("dp", [P, SLOTS], F32)
+        for lo, hi in ((0, 256), (256, SLOTS)):
+            nc.scalar.activation(dp[:, lo:hi], c0[:, lo:hi], ACT.Identity, bias=dz[:], scale=dp_scale[:])
+            nc.vector.tensor_tensor(placed[:].indirect(offsets[:, lo // 16:hi // 16]), dp[:, lo:hi], twice_sig[:, lo:hi], ALU.mult)
+
+        for s in range(POOL // STORE):
+            cols = slice(s * STORE, (s + 1) * STORE)
+            total = sbuf(f"total{s}", [P, STORE], F32)
+            nc.vector.tensor_tensor(total[:], placed[:, cols], old_sb[:, cols], ALU.add)
+            nc.sync.dma_start(out=out[:, cols], in_=total[:])

@@ -54,8 +54,11 @@ def tile_attend_blrcentred_capped_kernel(tc, query, keys_words, keys_scales, th,
 
         offsets = sbuf("offsets", [P, SLOTS // 16], U16)
         tab_plane = sbuf("tab_plane", [P, POOL], U8)
-        keys_plane = sbuf("keys_plane", [P, POOL], U8)
         tab_pool = sbuf("tab_pool", [P, POOL], I32)
+        keys_plane = sbuf("keys_plane", [P, POOL], U8)
+        keys_pool = sbuf("keys_pool", [P, POOL], I32)
+        g_raw = sbuf("g_raw", [P, PACK, ROWS], F32)
+        old_sb = sbuf("old_sb", [P, POOL], F32)
         placed = sbuf("placed", [P, POOL], F32)
         w_raw = sbuf("w_raw", [P, PACK, HIDDEN], F32)
         q_raw = sbuf("q_raw", [P, PACK, ROWS], F32)
@@ -64,51 +67,69 @@ def tile_attend_blrcentred_capped_kernel(tc, query, keys_words, keys_scales, th,
         th_sb = sbuf("th_sb", [P, 1], F32)
         reserve_sb = sbuf("reserve_sb", [P, 1], F32)
 
-        nc.vector.memset(tab_plane[:].bitcast(I32), 0)
         nc.vector.memset(keys_plane[:].bitcast(I32), 0)
+        nc.vector.memset(tab_plane[:].bitcast(I32), 0)
         nc.vector.memset(placed[:], 0.0)
 
+        load_words(keys_pool, keys_words)
         nc.sync.dma_start(offsets[:], offs)
-        nc.sync.dma_start(out=w_raw[:], in_=w1.rearrange("(p j) c -> p j c", j=PACK))
-        load_words(tab_pool, tab_words)
         nc.sync.dma_start(out=q_raw[:], in_=query.rearrange("(p j) q -> p j q", j=PACK))
-        load_scale_rows(nc.scalar, tab_plane, tab_scales)
-        load_scale_rows(nc.gpsimd, keys_plane, keys_scales)
-        nc.gpsimd.dma_start(out=share_sb[:], in_=share.rearrange("(p t) o -> p (t o)", t=PACK))
+        load_scale_rows(nc.sync, keys_plane, keys_scales)
+        nc.sync.dma_start(out=w_raw[:], in_=w1.rearrange("(p j) c -> p j c", j=PACK))
+        load_scale_rows(nc.sync, tab_plane, tab_scales)
+        load_words(tab_pool, tab_words)
+        nc.sync.dma_start(out=reserve_sb[:], in_=reserve)
+        nc.sync.dma_start(out=hsc_sb[:], in_=hsc.rearrange("(p t) o -> p (t o)", t=PACK))
+        nc.sync.dma_start(out=g_raw[:], in_=gout.rearrange("(p j) q -> p j q", j=PACK))
+        nc.sync.dma_start(out=old_sb[:], in_=old)
         nc.gpsimd.dma_start(out=th_sb[:], in_=th)
-        nc.gpsimd.dma_start(out=hsc_sb[:], in_=hsc.rearrange("(p t) o -> p (t o)", t=PACK))
-        nc.gpsimd.dma_start(out=reserve_sb[:], in_=reserve)
+        nc.gpsimd.dma_start(out=share_sb[:], in_=share.rearrange("(p t) o -> p (t o)", t=PACK))
+        half_th = sbuf("half_th", [P, 1], F32)
+        nc.gpsimd.tensor_scalar(half_th[:], th_sb[:], -0.5, 0.0, ALU.mult, ALU.add)
+        share_mean = sbuf("share_mean", [P, PACK], F32)
+        nc.gpsimd.tensor_scalar(share_mean[:], share_sb[:], 1.0 / PAGE, 0.0, ALU.mult, ALU.add)
 
-        tab_scale = sbuf("tab_scale", [P, SLOTS], U8)
-        nc.vector.tensor_copy(tab_scale[:], tab_plane[:].indirect(offsets[:]))
+        def group_rows(raw, name, slot=None):
+            grouped = sbuf(name, [P, ROWS, PACK], BF16, tag=slot)
+            nc.scalar.copy(grouped[:].rearrange("p (c i) j -> p c j i", i=4), raw[:].rearrange("p j (c i) -> p c j i", i=4))
+            return grouped
 
+        q_grouped = group_rows(q_raw, "q_grouped")
+        q_codes = sbuf("q_codes", [P, ROWS], U32)
+        q_scale = sbuf("q_scale", [P, ROWS], U8)
+        quantize(q_codes[:], q_scale[:], q_grouped[:].rearrange("p q j -> p (q j)"))
+        keys_codes = sbuf("keys_codes", [P, SLOTS], U32)
+        nc.vector.tensor_copy(keys_codes[:], keys_pool[:].bitcast(U32).indirect(offsets[:]))
+        keys_scale = sbuf("keys_scale", [P, SLOTS], U8)
+        nc.vector.tensor_copy(keys_scale[:], keys_plane[:].indirect(offsets[:]))
+        score = ps.tile([P, SLOTS], F32, name="score")
+        product(score[:], q_codes[:], q_scale[:], keys_codes[:], keys_scale[:])
         w_grouped = sbuf("w_grouped", [P, PACK, P, PACK], BF16)
         w_dst = w_grouped[:].rearrange("p t m j -> p m j t")
         w_src = w_raw[:].rearrange("p j (m t) -> p m j t", t=PACK)
         nc.scalar.copy(w_dst[:, 0:80], w_src[:, 0:80])
         nc.vector.tensor_copy(w_dst[:, 80:128], w_src[:, 80:128])
-        keys_pool = sbuf("keys_pool", [P, POOL], I32, tag="w_raw")
-        load_words(keys_pool, keys_words)
-        keys_scale = sbuf("keys_scale", [P, SLOTS], U8)
-        nc.vector.tensor_copy(keys_scale[:], keys_plane[:].indirect(offsets[:]))
+        halves = sbuf("halves", [P, 2 * SLOTS], F32, tag="w_raw")
+        tanh_half = halves[:, 0:SLOTS]
+        relu_half = halves[:, SLOTS:2 * SLOTS]
+        nc.scalar.activation(tanh_half, score[:], ACT.Tanh, bias=half_th[:], scale=0.5)
+        nc.scalar.activation(relu_half, score[:], ACT.Relu, bias=half_th[:], scale=0.5)
+        tanh_abs = sbuf("tanh_abs", [P, SLOTS], F32)
+        nc.scalar.activation(tanh_abs[:], tanh_half, ACT.Abs)
+
+        log_sig = sbuf("log_sig", [P, SLOTS], F32)
+        nc.scalar.activation(log_sig[:], tanh_abs[:], ACT.Ln, bias=0.5, scale=0.5)
+        tab_scale = sbuf("tab_scale", [P, SLOTS], U8)
+        nc.vector.tensor_copy(tab_scale[:], tab_plane[:].indirect(offsets[:]))
+
         w_codes = sbuf("w_codes", [P, HIDDEN], U32)
         w_scale = sbuf("w_scale", [P, HIDDEN], U8)
         quantize(w_codes[:], w_scale[:], w_grouped[:].rearrange("p t m j -> p (t m j)"))
-
-        share_mean = sbuf("share_mean", [P, PACK], F32)
-        half_th = sbuf("half_th", [P, 1], F32)
 
         tab_codes = sbuf("tab_codes", [P, SLOTS], U32)
         for h in range(2):
             nc.vector.tensor_copy(tab_codes[:, 256 * h:256 * (h + 1)],
                                   tab_pool[:].bitcast(U32).indirect(offsets[:, 16 * h:16 * (h + 1)]))
-        old_sb = sbuf("old_sb", [P, POOL], F32, tag="tab_pool")
-        nc.vector.tensor_scalar(share_mean[:], share_sb[:], 1.0 / PAGE, None, ALU.mult)
-
-        def group_rows(raw, name):
-            grouped = sbuf(name, [P, ROWS, PACK], BF16)
-            nc.scalar.copy(grouped[:].rearrange("p (c i) j -> p c j i", i=4), raw[:].rearrange("p j (c i) -> p c j i", i=4))
-            return grouped
 
         def layer(c):
             cols = slice(c * CHUNK, (c + 1) * CHUNK)
@@ -119,75 +140,62 @@ def tile_attend_blrcentred_capped_kernel(tc, query, keys_words, keys_scales, th,
             sums = sbuf(f"sums{c}", [P, PAGES, PACK], F32)
             nc.vector.tensor_reduce(sums[:], zh[:].rearrange("p t (g j) -> p g t j", j=PAGE), AX.X, ALU.add)
             shift = sbuf(f"shift{c}", [P, PAGES, PACK], F32)
-            nc.vector.tensor_tensor(shift[:], sums[:], share_mean[:].unsqueeze(1).to_broadcast([P, PAGES, PACK]), ALU.mult)
-            centred = sbuf(f"centred{c}", [P, PAGES, PAGE, PACK], F32)
-            nc.vector.tensor_tensor(centred[:], zh[:].rearrange("p t (g j) -> p g j t", j=PAGE),
-                                    shift[:].unsqueeze(2).to_broadcast([P, PAGES, PAGE, PACK]), ALU.subtract)
-            hv = sbuf(f"hv{c}", [P, CHUNK, PACK], F32)
-            nc.scalar.activation(hv[:].rearrange("p i t -> p (i t)"), centred[:].rearrange("p g j t -> p (g j t)"), ACT.Tanh)
-            return hv
+            nc.gpsimd.tensor_tensor(shift[:], sums[:], share_mean[:].unsqueeze(1).to_broadcast([P, PAGES, PACK]), ALU.mult)
+            centred = sbuf(f"centred{c}", [P, CHUNK * PACK], F32)
+            if c < CHUNKS - 1:
+                nc.vector.tensor_tensor(centred[:].rearrange("p (g j t) -> p g j t", j=PAGE, t=PACK),
+                                        zh[:].rearrange("p t (g j) -> p g j t", j=PAGE),
+                                        shift[:].unsqueeze(2).to_broadcast([P, PAGES, PAGE, PACK]), ALU.subtract)
+            else:
+                nc.vector.tensor_tensor(centred[:].rearrange("p (t g j) -> p t g j", j=PAGE, t=PACK),
+                                        zh[:].rearrange("p t (g j) -> p t g j", j=PAGE),
+                                        shift[:].rearrange("p g t -> p t g").unsqueeze(3).to_broadcast([P, PACK, PAGES, PAGE]),
+                                        ALU.subtract)
+            hv = sbuf(f"hv{c}", [P, CHUNK * PACK], F32)
+            nc.scalar.activation(hv[:], centred[:], ACT.Tanh)
+            hs = sbuf(f"hs{c}", [P, CHUNK, PACK], BF16)
+            if c == CHUNKS - 1:
+                for t in range(PACK):
+                    nc.scalar.activation(hs[:, :, t], hv[:, t * CHUNK:(t + 1) * CHUNK], ACT.Copy, scale=hsc_sb[:, t:t + 1])
+            return hv, hs
 
-        hvs = [layer(0), layer(1)]
+        hvs = [layer(c) for c in range(CHUNKS)]
+        twice_sig = sbuf("twice_sig", [P, SLOTS], F32, tag="centred3")
+        nc.scalar.activation(twice_sig[:], tanh_half, ACT.Identity, bias=1.0)
 
-        q_grouped = group_rows(q_raw, "q_grouped")
-        g_raw = sbuf("g_raw", [P, PACK, ROWS], F32, tag="q_raw")
-        nc.sync.dma_start(out=g_raw[:], in_=gout.rearrange("(p j) q -> p j q", j=PACK))
-        nc.sync.dma_start(out=old_sb[:], in_=old)
-        q_codes = sbuf("q_codes", [P, ROWS], U32)
-        q_scale = sbuf("q_scale", [P, ROWS], U8)
-        quantize(q_codes[:], q_scale[:], q_grouped[:].rearrange("p q j -> p (q j)"))
-        keys_codes = sbuf("keys_codes", [P, SLOTS], U32)
-        nc.vector.tensor_copy(keys_codes[:], keys_pool[:].bitcast(U32).indirect(offsets[:]))
-        nc.vector.tensor_scalar(half_th[:], th_sb[:], -0.5, None, ALU.mult)
-        score = ps.tile([P, SLOTS], F32, name="score")
-        product(score[:], q_codes[:], q_scale[:], keys_codes[:], keys_scale[:])
-        tanh_half = sbuf("tanh_half", [P, SLOTS], F32)
-        nc.scalar.activation(tanh_half[:], score[:], ACT.Tanh, bias=half_th[:], scale=0.5)
-        relu_half = sbuf("relu_half", [P, SLOTS], F32)
-        relu_sum = sbuf("relu_sum", [P, 1], F32)
-        nc.scalar.activation(relu_half[:], score[:], ACT.Relu, bias=half_th[:], scale=0.5, accum_out=relu_sum[:])
-        tanh_abs = sbuf("tanh_abs", [P, SLOTS], F32)
-        nc.scalar.activation(tanh_abs[:], tanh_half[:], ACT.Abs)
 
-        hvs = hvs + [layer(2), layer(3)]
-
-        g_grouped = group_rows(g_raw, "g_grouped")
+        g_grouped = group_rows(g_raw, "g_grouped", "tanh_abs")
         g_codes = sbuf("g_codes", [P, ROWS], U32)
         g_scale = sbuf("g_scale", [P, ROWS], U8)
         quantize(g_codes[:], g_scale[:], g_grouped[:].rearrange("p q j -> p (q j)"))
-        z_part = sbuf("z_part", [P, 1], F32)
-        nc.vector.scalar_tensor_tensor(z_part[:], relu_sum[:], 2.0, reserve_sb[:], ALU.mult, ALU.add)
-
-        log_sig = sbuf("log_sig", [P, SLOTS], F32)
-        log_sum = sbuf("log_sum", [P, 1], F32)
-        nc.scalar.activation(log_sig[:], tanh_abs[:], ACT.Ln, bias=0.5, scale=0.5, accum_out=log_sum[:])
-        twice_sig = sbuf("twice_sig", [P, SLOTS], F32)
-        nc.scalar.activation(twice_sig[:], tanh_half[:], ACT.Identity, bias=1.0)
-
-        c0 = ps.tile([P, SLOTS], F32, name="c0")
-        hs_tiles = []
-        for c in range(CHUNKS):
-            hs = sbuf(f"hs{c}", [P, CHUNK, PACK], BF16)
-            nc.vector.tensor_tensor(hs[:], hvs[c][:], hsc_sb[:].unsqueeze(1).to_broadcast([P, CHUNK, PACK]), ALU.mult)
-            hs_tiles.append(hs)
-            if c >= 1:
-                finish = [c - 1] if c < CHUNKS - 1 else [c - 1, c]
-                for d in finish:
-                    hs_codes = sbuf(f"hs_codes{d}", [P, CHUNK], U32)
-                    hs_scale = sbuf(f"hs_scale{d}", [P, CHUNK], U8)
-                    quantize(hs_codes[:], hs_scale[:], hs_tiles[d][:].rearrange("p i t -> p (i t)"))
-                    product(c0[:, d * CHUNK:(d + 1) * CHUNK], g_codes[:], g_scale[:], hs_codes[:], hs_scale[:])
-
+        soft = sbuf("soft", [P, SLOTS], F32, tag="centred1")
+        soft_sum = sbuf("soft_sum", [P, 1], F32)
+        nc.vector.scalar_tensor_tensor(soft[:], relu_half, 2.0, log_sig[:], ALU.mult, ALU.subtract, accum_out=soft_sum[:])
         z = sbuf("z", [P, 1], F32)
-        nc.vector.tensor_tensor(z[:], z_part[:], log_sum[:], ALU.subtract)
-        soft = sbuf("soft", [P, SLOTS], F32)
-        nc.vector.scalar_tensor_tensor(soft[:], relu_half[:], 2.0, log_sig[:], ALU.mult, ALU.subtract)
+        nc.gpsimd.tensor_tensor(z[:], soft_sum[:], reserve_sb[:], ALU.add)
         z_inv = sbuf("z_inv", [P, 1], F32)
         nc.vector.reciprocal(z_inv[:], z[:])
         dz_factor = sbuf("dz_factor", [P, 1], F32)
-        nc.vector.tensor_scalar(dz_factor[:], z_inv[:], z_inv[:], -256.0, ALU.mult, ALU.mult)
+        nc.gpsimd.tensor_scalar(dz_factor[:], z_inv[:], z_inv[:], -256.0, ALU.mult, ALU.mult)
         dp_scale = sbuf("dp_scale", [P, 1], F32)
-        nc.vector.tensor_scalar(dp_scale[:], z_inv[:], 256.0, None, ALU.mult)
+        nc.gpsimd.tensor_scalar(dp_scale[:], z_inv[:], 256.0, 0.0, ALU.mult, ALU.add)
+        c0 = ps.tile([P, SLOTS], F32, name="c0")
+        def scale_hidden(c):
+            hv, hs = hvs[c]
+            nc.vector.tensor_tensor(hs[:], hv[:].rearrange("p (i t) -> p i t", t=PACK),
+                                    hsc_sb[:].unsqueeze(1).to_broadcast([P, CHUNK, PACK]), ALU.mult)
+
+        def read_product(c):
+            hs_codes = sbuf(f"hs_codes{c}", [P, CHUNK], U32)
+            hs_scale = sbuf(f"hs_scale{c}", [P, CHUNK], U8)
+            quantize(hs_codes[:], hs_scale[:], hvs[c][1][:].rearrange("p i t -> p (i t)"))
+            product(c0[:, c * CHUNK:(c + 1) * CHUNK], g_codes[:], g_scale[:], hs_codes[:], hs_scale[:])
+
+        for c in range(CHUNKS - 1):
+            scale_hidden(c)
+        for c in range(CHUNKS):
+            read_product(c)
+
         dz_terms = sbuf("dz_terms", [P, SLOTS], F32)
         dz = sbuf("dz", [P, 1], F32)
         nc.vector.scalar_tensor_tensor(dz_terms[:], c0[:], dz_factor[:], soft[:], ALU.mult, ALU.mult, accum_out=dz[:])
@@ -197,8 +205,7 @@ def tile_attend_blrcentred_capped_kernel(tc, query, keys_words, keys_scales, th,
             nc.scalar.activation(dp[:, lo:hi], c0[:, lo:hi], ACT.Identity, bias=dz[:], scale=dp_scale[:])
             nc.vector.tensor_tensor(placed[:].indirect(offsets[:, lo // 16:hi // 16]), dp[:, lo:hi], twice_sig[:, lo:hi], ALU.mult)
 
-        for s in range(POOL // STORE):
-            cols = slice(s * STORE, (s + 1) * STORE)
-            total = sbuf(f"total{s}", [P, STORE], F32)
-            nc.vector.tensor_tensor(total[:], placed[:, cols], old_sb[:, cols], ALU.add)
-            nc.sync.dma_start(out=out[:, cols], in_=total[:])
+        for lo, hi in ((0, 256), (256, 768), (768, 1280), (1280, 1792), (1792, POOL)):
+            total = sbuf(f"total{lo}", [P, hi - lo], F32)
+            nc.vector.tensor_tensor(total[:], placed[:, lo:hi], old_sb[:, lo:hi], ALU.add)
+            nc.sync.dma_start(out=out[:, lo:hi], in_=total[:])

@@ -85,9 +85,7 @@ def tile_attend_blrcentred_capped_kernel(tc, query, keys_words, keys_scales, th,
         nc.gpsimd.dma_start(out=th_sb[:], in_=th)
         nc.gpsimd.dma_start(out=share_sb[:], in_=share.rearrange("(p t) o -> p (t o)", t=PACK))
         half_th = sbuf("half_th", [P, 1], F32)
-        nc.gpsimd.tensor_scalar(half_th[:], th_sb[:], -0.5, 0.0, ALU.mult, ALU.add)
-        share_mean = sbuf("share_mean", [P, PACK], F32)
-        nc.gpsimd.tensor_scalar(share_mean[:], share_sb[:], 1.0 / PAGE, 0.0, ALU.mult, ALU.add)
+        nc.scalar.activation(half_th[:], th_sb[:], ACT.Copy, scale=-0.5)
 
         def group_rows(raw, name, slot=None):
             grouped = sbuf(name, [P, ROWS, PACK], BF16, tag=slot)
@@ -140,7 +138,8 @@ def tile_attend_blrcentred_capped_kernel(tc, query, keys_words, keys_scales, th,
             sums = sbuf(f"sums{c}", [P, PAGES, PACK], F32)
             nc.vector.tensor_reduce(sums[:], zh[:].rearrange("p t (g j) -> p g t j", j=PAGE), AX.X, ALU.add)
             shift = sbuf(f"shift{c}", [P, PAGES, PACK], F32)
-            nc.gpsimd.tensor_tensor(shift[:], sums[:], share_mean[:].unsqueeze(1).to_broadcast([P, PAGES, PACK]), ALU.mult)
+            nc.vector.scalar_tensor_tensor(shift[:], sums[:], 1.0 / PAGE,
+                                           share_sb[:].unsqueeze(1).to_broadcast([P, PAGES, PACK]), ALU.mult, ALU.mult)
             centred = sbuf(f"centred{c}", [P, CHUNK * PACK], F32)
             if c < CHUNKS - 1:
                 nc.vector.tensor_tensor(centred[:].rearrange("p (g j t) -> p g j t", j=PAGE, t=PACK),
@@ -160,6 +159,17 @@ def tile_attend_blrcentred_capped_kernel(tc, query, keys_words, keys_scales, th,
             return hv, hs
 
         hvs = [layer(c) for c in range(CHUNKS)]
+        neg_soft = sbuf("neg_soft", [P, SLOTS], F32, tag="centred1")
+        neg_sum = sbuf("neg_sum", [P, 1], F32)
+        nc.vector.scalar_tensor_tensor(neg_soft[:], relu_half, -2.0, log_sig[:], ALU.mult, ALU.add, accum_out=neg_sum[:])
+        z = sbuf("z", [P, 1], F32)
+        nc.vector.tensor_tensor(z[:], reserve_sb[:], neg_sum[:], ALU.subtract)
+        z_inv = sbuf("z_inv", [P, 1], F32)
+        nc.vector.reciprocal(z_inv[:], z[:])
+        dz_factor = sbuf("dz_factor", [P, 1], F32)
+        nc.scalar.activation(dz_factor[:], z_inv[:], ACT.Square, scale=16.0)
+        dp_scale = sbuf("dp_scale", [P, 1], F32)
+        nc.scalar.activation(dp_scale[:], z_inv[:], ACT.Copy, scale=256.0)
         twice_sig = sbuf("twice_sig", [P, SLOTS], F32, tag="centred3")
         nc.scalar.activation(twice_sig[:], tanh_half, ACT.Identity, bias=1.0)
 
@@ -168,17 +178,6 @@ def tile_attend_blrcentred_capped_kernel(tc, query, keys_words, keys_scales, th,
         g_codes = sbuf("g_codes", [P, ROWS], U32)
         g_scale = sbuf("g_scale", [P, ROWS], U8)
         quantize(g_codes[:], g_scale[:], g_grouped[:].rearrange("p q j -> p (q j)"))
-        soft = sbuf("soft", [P, SLOTS], F32, tag="centred1")
-        soft_sum = sbuf("soft_sum", [P, 1], F32)
-        nc.vector.scalar_tensor_tensor(soft[:], relu_half, 2.0, log_sig[:], ALU.mult, ALU.subtract, accum_out=soft_sum[:])
-        z = sbuf("z", [P, 1], F32)
-        nc.gpsimd.tensor_tensor(z[:], soft_sum[:], reserve_sb[:], ALU.add)
-        z_inv = sbuf("z_inv", [P, 1], F32)
-        nc.vector.reciprocal(z_inv[:], z[:])
-        dz_factor = sbuf("dz_factor", [P, 1], F32)
-        nc.gpsimd.tensor_scalar(dz_factor[:], z_inv[:], z_inv[:], -256.0, ALU.mult, ALU.mult)
-        dp_scale = sbuf("dp_scale", [P, 1], F32)
-        nc.gpsimd.tensor_scalar(dp_scale[:], z_inv[:], 256.0, 0.0, ALU.mult, ALU.add)
         c0 = ps.tile([P, SLOTS], F32, name="c0")
         def scale_hidden(c):
             hv, hs = hvs[c]
@@ -198,7 +197,7 @@ def tile_attend_blrcentred_capped_kernel(tc, query, keys_words, keys_scales, th,
 
         dz_terms = sbuf("dz_terms", [P, SLOTS], F32)
         dz = sbuf("dz", [P, 1], F32)
-        nc.vector.scalar_tensor_tensor(dz_terms[:], c0[:], dz_factor[:], soft[:], ALU.mult, ALU.mult, accum_out=dz[:])
+        nc.vector.scalar_tensor_tensor(dz_terms[:], c0[:], dz_factor[:], neg_soft[:], ALU.mult, ALU.mult, accum_out=dz[:])
 
         dp = sbuf("dp", [P, SLOTS], F32)
         for lo, hi in ((0, 256), (256, SLOTS)):

@@ -15,15 +15,19 @@ AX = mybir.AxisListType
 
 P = 128
 PACK = 4
+QUADRANT = 32
+SCALE_ROWS = 16
+LIST_ROWS = 16
 POOL = 2048
 SLOTS = 512
 ROWS = 128
 HIDDEN = 512
 PAGE = 16
 CHUNK = 128
-CHUNKS = SLOTS // CHUNK
 PAGES = CHUNK // PAGE
-STORE = 512
+HALF = SLOTS // 2
+W_SCALAR = 80
+STORE_EDGES = (0, 256, 768, 1280, 1792, POOL)
 
 FLOPS = 2 * 512 * SLOTS * (ROWS + HIDDEN + ROWS)
 
@@ -38,12 +42,19 @@ def tile_attend_blrcentred_capped_kernel(tc, query, keys_words, keys_scales, th,
         def sbuf(name, shape, dtype, tag=None):
             return sb.tile(shape, dtype, name=name, tag=tag or name, align_bytes=64)
 
-        def load_scale_rows(queue, plane, scales):
+        def load_scale_rows(plane, scales):
             for j in range(PACK):
-                queue.dma_start(out=plane[j:P:32, :].bitcast(I32), in_=scales[0, j:16:PACK, :].bitcast(I32))
+                nc.sync.dma_start(out=plane[j:P:QUADRANT, :].bitcast(I32),
+                                  in_=scales[0, j:SCALE_ROWS:PACK, :].bitcast(I32))
 
         def load_words(pool_words, words):
             nc.sync.dma_start(out=pool_words[:], in_=words[0].rearrange("p n t -> p (n t)").bitcast(I32))
+
+        def listed(lo, hi):
+            return offsets[:, lo // LIST_ROWS:hi // LIST_ROWS]
+
+        def interleaved(grouped, raw):
+            return grouped[:].rearrange("p (c i) j -> p c j i", i=4), raw[:].rearrange("p j (c i) -> p c j i", i=4)
 
         def quantize(codes, scales, grouped):
             nc.vector.quantize_mx(out=codes.bitcast(FP8X4), scales=scales, in_=grouped)
@@ -52,7 +63,7 @@ def tile_attend_blrcentred_capped_kernel(tc, query, keys_words, keys_scales, th,
             nc.tensor.matmul_mx(out=acc, lhsT=lhs_codes.bitcast(FP8X4), lhsT_scale=lhs_scales,
                                 rhs=rhs_codes.bitcast(FP8X4), rhs_scale=rhs_scales, start=True, stop=True)
 
-        offsets = sbuf("offsets", [P, SLOTS // 16], U16)
+        offsets = sbuf("offsets", [P, SLOTS // LIST_ROWS], U16)
         tab_plane = sbuf("tab_plane", [P, POOL], U8)
         tab_pool = sbuf("tab_pool", [P, POOL], I32)
         keys_plane = sbuf("keys_plane", [P, POOL], U8)
@@ -67,144 +78,170 @@ def tile_attend_blrcentred_capped_kernel(tc, query, keys_words, keys_scales, th,
         th_sb = sbuf("th_sb", [P, 1], F32)
         reserve_sb = sbuf("reserve_sb", [P, 1], F32)
 
-        nc.vector.memset(keys_plane[:].bitcast(I32), 0)
         nc.vector.memset(tab_plane[:].bitcast(I32), 0)
+        nc.vector.memset(keys_plane[:].bitcast(I32), 0)
         nc.vector.memset(placed[:], 0.0)
 
-        load_words(keys_pool, keys_words)
         nc.sync.dma_start(offsets[:], offs)
-        nc.sync.dma_start(out=q_raw[:], in_=query.rearrange("(p j) q -> p j q", j=PACK))
-        load_scale_rows(nc.sync, keys_plane, keys_scales)
+        nc.sync.dma_start(out=share_sb[:], in_=share.rearrange("(p t) o -> p (t o)", t=PACK))
         nc.sync.dma_start(out=w_raw[:], in_=w1.rearrange("(p j) c -> p j c", j=PACK))
-        load_scale_rows(nc.sync, tab_plane, tab_scales)
+        load_scale_rows(tab_plane, tab_scales)
         load_words(tab_pool, tab_words)
-        nc.sync.dma_start(out=reserve_sb[:], in_=reserve)
-        nc.sync.dma_start(out=hsc_sb[:], in_=hsc.rearrange("(p t) o -> p (t o)", t=PACK))
+        nc.sync.dma_start(out=q_raw[:], in_=query.rearrange("(p j) q -> p j q", j=PACK))
+        load_words(keys_pool, keys_words)
+        load_scale_rows(keys_plane, keys_scales)
+        nc.gpsimd.dma_start(out=hsc_sb[:], in_=hsc.rearrange("(p t) o -> p (t o)", t=PACK))
+        nc.sync.dma_start(out=th_sb[:], in_=th)
         nc.sync.dma_start(out=g_raw[:], in_=gout.rearrange("(p j) q -> p j q", j=PACK))
+        nc.sync.dma_start(out=reserve_sb[:], in_=reserve)
         nc.sync.dma_start(out=old_sb[:], in_=old)
-        nc.gpsimd.dma_start(out=th_sb[:], in_=th)
-        nc.gpsimd.dma_start(out=share_sb[:], in_=share.rearrange("(p t) o -> p (t o)", t=PACK))
-        half_th = sbuf("half_th", [P, 1], F32)
-        nc.scalar.activation(half_th[:], th_sb[:], ACT.Copy, scale=-0.5)
 
-        def group_rows(raw, name, slot=None):
-            grouped = sbuf(name, [P, ROWS, PACK], BF16, tag=slot)
-            nc.scalar.copy(grouped[:].rearrange("p (c i) j -> p c j i", i=4), raw[:].rearrange("p j (c i) -> p c j i", i=4))
-            return grouped
-
-        q_grouped = group_rows(q_raw, "q_grouped")
-        q_codes = sbuf("q_codes", [P, ROWS], U32)
-        q_scale = sbuf("q_scale", [P, ROWS], U8)
-        quantize(q_codes[:], q_scale[:], q_grouped[:].rearrange("p q j -> p (q j)"))
-        keys_codes = sbuf("keys_codes", [P, SLOTS], U32)
-        nc.vector.tensor_copy(keys_codes[:], keys_pool[:].bitcast(U32).indirect(offsets[:]))
-        keys_scale = sbuf("keys_scale", [P, SLOTS], U8)
-        nc.vector.tensor_copy(keys_scale[:], keys_plane[:].indirect(offsets[:]))
-        score = ps.tile([P, SLOTS], F32, name="score")
-        product(score[:], q_codes[:], q_scale[:], keys_codes[:], keys_scale[:])
         w_grouped = sbuf("w_grouped", [P, PACK, P, PACK], BF16)
         w_dst = w_grouped[:].rearrange("p t m j -> p m j t")
         w_src = w_raw[:].rearrange("p j (m t) -> p m j t", t=PACK)
-        nc.scalar.copy(w_dst[:, 0:80], w_src[:, 0:80])
-        nc.vector.tensor_copy(w_dst[:, 80:128], w_src[:, 80:128])
-        halves = sbuf("halves", [P, 2 * SLOTS], F32, tag="w_raw")
-        tanh_half = halves[:, 0:SLOTS]
-        relu_half = halves[:, SLOTS:2 * SLOTS]
-        nc.scalar.activation(tanh_half, score[:], ACT.Tanh, bias=half_th[:], scale=0.5)
-        nc.scalar.activation(relu_half, score[:], ACT.Relu, bias=half_th[:], scale=0.5)
-        tanh_abs = sbuf("tanh_abs", [P, SLOTS], F32)
-        nc.scalar.activation(tanh_abs[:], tanh_half, ACT.Abs)
-
-        log_sig = sbuf("log_sig", [P, SLOTS], F32)
-        nc.scalar.activation(log_sig[:], tanh_abs[:], ACT.Ln, bias=0.5, scale=0.5)
+        nc.scalar.copy(w_dst[:, 0:W_SCALAR], w_src[:, 0:W_SCALAR])
+        nc.vector.tensor_copy(w_dst[:, W_SCALAR:P], w_src[:, W_SCALAR:P])
         tab_scale = sbuf("tab_scale", [P, SLOTS], U8)
         nc.vector.tensor_copy(tab_scale[:], tab_plane[:].indirect(offsets[:]))
-
         w_codes = sbuf("w_codes", [P, HIDDEN], U32)
         w_scale = sbuf("w_scale", [P, HIDDEN], U8)
         quantize(w_codes[:], w_scale[:], w_grouped[:].rearrange("p t m j -> p (t m j)"))
-
         tab_codes = sbuf("tab_codes", [P, SLOTS], U32)
-        for h in range(2):
-            nc.vector.tensor_copy(tab_codes[:, 256 * h:256 * (h + 1)],
-                                  tab_pool[:].bitcast(U32).indirect(offsets[:, 16 * h:16 * (h + 1)]))
+        for lo in range(0, SLOTS, HALF):
+            nc.vector.tensor_copy(tab_codes[:, lo:lo + HALF], tab_pool[:].bitcast(U32).indirect(listed(lo, lo + HALF)))
 
-        def layer(c):
+        def layer_product(c):
             cols = slice(c * CHUNK, (c + 1) * CHUNK)
             zh = ps.tile([P, PACK, CHUNK], F32, name=f"zh{c}")
             for t in range(PACK):
                 feats = slice(t * P, (t + 1) * P)
                 product(zh[:, t, :], w_codes[:, feats], w_scale[:, feats], tab_codes[:, cols], tab_scale[:, cols])
-            sums = sbuf(f"sums{c}", [P, PAGES, PACK], F32)
-            nc.vector.tensor_reduce(sums[:], zh[:].rearrange("p t (g j) -> p g t j", j=PAGE), AX.X, ALU.add)
-            shift = sbuf(f"shift{c}", [P, PAGES, PACK], F32)
-            nc.vector.scalar_tensor_tensor(shift[:], sums[:], 1.0 / PAGE,
-                                           share_sb[:].unsqueeze(1).to_broadcast([P, PAGES, PACK]), ALU.mult, ALU.mult)
-            centred = sbuf(f"centred{c}", [P, CHUNK * PACK], F32)
-            if c < CHUNKS - 1:
-                nc.vector.tensor_tensor(centred[:].rearrange("p (g j t) -> p g j t", j=PAGE, t=PACK),
-                                        zh[:].rearrange("p t (g j) -> p g j t", j=PAGE),
-                                        shift[:].unsqueeze(2).to_broadcast([P, PAGES, PAGE, PACK]), ALU.subtract)
-            else:
-                nc.vector.tensor_tensor(centred[:].rearrange("p (t g j) -> p t g j", j=PAGE, t=PACK),
-                                        zh[:].rearrange("p t (g j) -> p t g j", j=PAGE),
-                                        shift[:].rearrange("p g t -> p t g").unsqueeze(3).to_broadcast([P, PACK, PAGES, PAGE]),
-                                        ALU.subtract)
-            hv = sbuf(f"hv{c}", [P, CHUNK * PACK], F32)
-            nc.scalar.activation(hv[:], centred[:], ACT.Tanh)
-            hs = sbuf(f"hs{c}", [P, CHUNK, PACK], BF16)
-            if c == CHUNKS - 1:
-                for t in range(PACK):
-                    nc.scalar.activation(hs[:, :, t], hv[:, t * CHUNK:(t + 1) * CHUNK], ACT.Copy, scale=hsc_sb[:, t:t + 1])
-            return hv, hs
+            return zh
 
-        hvs = [layer(c) for c in range(CHUNKS)]
-        neg_soft = sbuf("neg_soft", [P, SLOTS], F32, tag="centred1")
-        neg_sum = sbuf("neg_sum", [P, 1], F32)
-        nc.vector.scalar_tensor_tensor(neg_soft[:], relu_half, -2.0, log_sig[:], ALU.mult, ALU.add, accum_out=neg_sum[:])
+        def page_sums(sums, zh):
+            nc.vector.tensor_reduce(sums, zh[:].rearrange("p t (g j) -> p g t j", j=PAGE), AX.X, ALU.add)
+
+        def page_shift(shift, sums, pages):
+            nc.vector.scalar_tensor_tensor(shift, sums, 1.0 / PAGE,
+                                           share_sb[:].unsqueeze(1).to_broadcast([P, pages, PACK]), ALU.mult, ALU.mult)
+
+        def centre_interleaved(centred, zh, shift):
+            nc.vector.tensor_tensor(centred[:], zh[:].rearrange("p t (g j) -> p g j t", j=PAGE),
+                                    shift.unsqueeze(2).to_broadcast([P, PAGES, PAGE, PACK]), ALU.subtract)
+
+        def scale_hidden(hs, hv, slots):
+            nc.vector.tensor_tensor(hs[:], hv[:], hsc_sb[:].unsqueeze(1).to_broadcast([P, slots, PACK]), ALU.mult)
+
+        zh0 = layer_product(0)
+        sums0 = sbuf("sums0", [P, PAGES, PACK], F32)
+        page_sums(sums0[:], zh0)
+        shift0 = sbuf("shift0", [P, PAGES, PACK], F32)
+        page_shift(shift0[:], sums0[:], PAGES)
+        centred0 = sbuf("centred0", [P, PACK, PAGES, PAGE], F32)
+        nc.vector.tensor_tensor(centred0[:], zh0[:].rearrange("p t (g j) -> p t g j", j=PAGE),
+                                shift0[:].rearrange("p g t -> p t g").unsqueeze(3).to_broadcast([P, PACK, PAGES, PAGE]),
+                                ALU.subtract)
+        hv0 = sbuf("hv0", [P, PACK, CHUNK], F32)
+        nc.scalar.activation(hv0[:].rearrange("p t i -> p (t i)"), centred0[:].rearrange("p t g j -> p (t g j)"), ACT.Tanh)
+        hs0 = sbuf("hs0", [P, CHUNK, PACK], BF16)
+        for t in range(PACK):
+            nc.scalar.activation(hs0[:, :, t], hv0[:, t, :], ACT.Copy, scale=hsc_sb[:, t:t + 1])
+
+        zh1 = layer_product(1)
+        sums1 = sbuf("sums1", [P, PAGES, PACK], F32)
+        page_sums(sums1[:], zh1)
+        shift1 = sbuf("shift1", [P, PAGES, PACK], F32)
+        page_shift(shift1[:], sums1[:], PAGES)
+        centred1 = sbuf("centred1", [P, PAGES, PAGE, PACK], F32)
+        centre_interleaved(centred1, zh1, shift1[:])
+        hv1 = sbuf("hv1", [P, CHUNK, PACK], F32)
+        nc.scalar.activation(hv1[:].rearrange("p i t -> p (i t)"), centred1[:].rearrange("p g j t -> p (g j t)"), ACT.Tanh)
+        g_grouped = sbuf("g_grouped", [P, ROWS, PACK], BF16, tag="centred1")
+        nc.scalar.copy(*interleaved(g_grouped, g_raw))
+
+        q_grouped = sbuf("q_grouped", [P, ROWS, PACK], BF16)
+        nc.scalar.copy(*interleaved(q_grouped, q_raw))
+        q_codes = sbuf("q_codes", [P, ROWS], U32)
+        q_scale = sbuf("q_scale", [P, ROWS], U8)
+        quantize(q_codes[:], q_scale[:], q_grouped[:].rearrange("p q j -> p (q j)"))
+        keys_codes = sbuf("keys_codes", [P, SLOTS], U32)
+        nc.vector.tensor_copy(keys_codes[:], keys_pool[:].bitcast(U32).indirect(offsets[:]))
+        keys_scale = sbuf("keys_scale", [P, SLOTS], U8, tag="keys_pool")
+        nc.vector.tensor_copy(keys_scale[:], keys_plane[:].indirect(offsets[:]))
+        score = ps.tile([P, SLOTS], F32, name="score")
+        product(score[:], q_codes[:], q_scale[:], keys_codes[:], keys_scale[:])
+        half_th = sbuf("half_th", [P, 1], F32, tag="shift1")
+        nc.scalar.activation(half_th[:], th_sb[:], ACT.Copy, scale=-0.5)
+        tanh_half = sbuf("tanh_half", [P, SLOTS], F32)
+        nc.scalar.activation(tanh_half[:], score[:], ACT.Tanh, bias=half_th[:], scale=0.5)
+        tanh_abs = sbuf("tanh_abs", [P, SLOTS], F32)
+        nc.scalar.activation(tanh_abs[:], tanh_half[:], ACT.Abs)
+
+        late_sums = sbuf("late_sums", [P, 2 * PAGES, PACK], F32, tag="keys_plane")
+        late_shift = sbuf("late_shift", [P, 2 * PAGES, PACK], F32)
+        late_hv = sbuf("late_hv", [P, HALF, PACK], F32)
+        late_zh = [layer_product(c) for c in range(HALF // CHUNK, SLOTS // CHUNK)]
+        for k in range(HALF // CHUNK):
+            page_sums(late_sums[:, k * PAGES:(k + 1) * PAGES], late_zh[k])
+        page_shift(late_shift[:], late_sums[:], 2 * PAGES)
+        for k in range(HALF // CHUNK):
+            centred = sbuf(f"centred{HALF // CHUNK + k}", [P, PAGES, PAGE, PACK], F32)
+            centre_interleaved(centred, late_zh[k], late_shift[:, k * PAGES:(k + 1) * PAGES])
+            nc.scalar.activation(late_hv[:, k * CHUNK:(k + 1) * CHUNK].rearrange("p i t -> p (i t)"),
+                                 centred[:].rearrange("p g j t -> p (g j t)"), ACT.Tanh)
+
+        log_sig = sbuf("log_sig", [P, SLOTS], F32, tag="centred3")
+        log_sum = sbuf("log_sum", [P, 1], F32)
+        nc.scalar.activation(log_sig[:], tanh_abs[:], ACT.Ln, bias=0.5, scale=0.5, accum_out=log_sum[:])
+        relu_half = sbuf("relu_half", [P, SLOTS], F32, tag="tanh_abs")
+        relu_sum = sbuf("relu_sum", [P, 1], F32)
+        nc.scalar.activation(relu_half[:], score[:], ACT.Relu, bias=half_th[:], scale=0.5, accum_out=relu_sum[:])
+        z_part = sbuf("z_part", [P, 1], F32)
+        nc.scalar.activation(z_part[:], log_sum[:], ACT.Identity, bias=reserve_sb[:], scale=-1.0)
         z = sbuf("z", [P, 1], F32)
-        nc.vector.tensor_tensor(z[:], reserve_sb[:], neg_sum[:], ALU.subtract)
-        z_inv = sbuf("z_inv", [P, 1], F32)
-        nc.vector.reciprocal(z_inv[:], z[:])
-        dz_factor = sbuf("dz_factor", [P, 1], F32)
-        nc.scalar.activation(dz_factor[:], z_inv[:], ACT.Square, scale=16.0)
-        dp_scale = sbuf("dp_scale", [P, 1], F32)
-        nc.scalar.activation(dp_scale[:], z_inv[:], ACT.Copy, scale=256.0)
-        twice_sig = sbuf("twice_sig", [P, SLOTS], F32, tag="centred3")
-        nc.scalar.activation(twice_sig[:], tanh_half, ACT.Identity, bias=1.0)
+        nc.scalar.activation(z[:], relu_sum[:], ACT.Identity, bias=z_part[:], scale=2.0)
+        sig = sbuf("sig", [P, SLOTS], F32, tag="log_sum")
+        nc.scalar.activation(sig[:], tanh_half[:], ACT.Identity, bias=256.0, scale=256.0)
 
-
-        g_grouped = group_rows(g_raw, "g_grouped", "tanh_abs")
-        g_codes = sbuf("g_codes", [P, ROWS], U32)
+        c0 = ps.tile([P, SLOTS], F32, name="c0")
+        g_codes = sbuf("g_codes", [P, ROWS], U32, tag="keys_pool")
         g_scale = sbuf("g_scale", [P, ROWS], U8)
         quantize(g_codes[:], g_scale[:], g_grouped[:].rearrange("p q j -> p (q j)"))
-        c0 = ps.tile([P, SLOTS], F32, name="c0")
-        def scale_hidden(c):
-            hv, hs = hvs[c]
-            nc.vector.tensor_tensor(hs[:], hv[:].rearrange("p (i t) -> p i t", t=PACK),
-                                    hsc_sb[:].unsqueeze(1).to_broadcast([P, CHUNK, PACK]), ALU.mult)
 
-        def read_product(c):
-            hs_codes = sbuf(f"hs_codes{c}", [P, CHUNK], U32)
-            hs_scale = sbuf(f"hs_scale{c}", [P, CHUNK], U8)
-            quantize(hs_codes[:], hs_scale[:], hvs[c][1][:].rearrange("p i t -> p (i t)"))
-            product(c0[:, c * CHUNK:(c + 1) * CHUNK], g_codes[:], g_scale[:], hs_codes[:], hs_scale[:])
+        def read_product(name, hs, lo, hi, tag=None):
+            codes = sbuf(name + "_codes", [P, hi - lo], U32, tag=tag)
+            scales = sbuf(name + "_scale", [P, hi - lo], U8)
+            quantize(codes[:], scales[:], hs[:].rearrange("p i t -> p (i t)"))
+            product(c0[:, lo:hi], g_codes[:], g_scale[:], codes[:], scales[:])
 
-        for c in range(CHUNKS - 1):
-            scale_hidden(c)
-        for c in range(CHUNKS):
-            read_product(c)
+        hs1 = sbuf("hs1", [P, CHUNK, PACK], BF16, tag="late_shift")
+        scale_hidden(hs1, hv1, CHUNK)
+        read_product("hs0", hs0, 0, CHUNK, tag="keys_plane")
+        late_hs = sbuf("late_hs", [P, HALF, PACK], BF16)
+        scale_hidden(late_hs, late_hv, HALF)
+        read_product("hs1", hs1, CHUNK, HALF)
+        read_product("late_hs", late_hs, HALF, SLOTS)
 
-        dz_terms = sbuf("dz_terms", [P, SLOTS], F32)
+        log_terms = sbuf("log_terms", [P, SLOTS], F32)
+        log_dot = sbuf("log_dot", [P, 1], F32)
+        nc.vector.scalar_tensor_tensor(log_terms[:], c0[:], 1.0, log_sig[:], ALU.mult, ALU.mult, accum_out=log_dot[:])
+        relu_terms = sbuf("relu_terms", [P, SLOTS], F32)
+        relu_dot = sbuf("relu_dot", [P, 1], F32)
+        nc.vector.scalar_tensor_tensor(relu_terms[:], c0[:], -2.0, relu_half[:], ALU.mult, ALU.mult, accum_out=relu_dot[:])
+        z_inv = sbuf("z_inv", [P, 1], F32)
+        nc.vector.reciprocal(z_inv[:], z[:])
+        dz_z = sbuf("dz_z", [P, 1], F32)
+        nc.vector.tensor_scalar(dz_z[:], log_dot[:], relu_dot[:], z_inv[:], ALU.add, ALU.mult)
         dz = sbuf("dz", [P, 1], F32)
-        nc.vector.scalar_tensor_tensor(dz_terms[:], c0[:], dz_factor[:], neg_soft[:], ALU.mult, ALU.mult, accum_out=dz[:])
+        nc.scalar.activation(dz[:], dz_z[:], ACT.Copy, scale=z_inv[:])
 
         dp = sbuf("dp", [P, SLOTS], F32)
-        for lo, hi in ((0, 256), (256, SLOTS)):
-            nc.scalar.activation(dp[:, lo:hi], c0[:, lo:hi], ACT.Identity, bias=dz[:], scale=dp_scale[:])
-            nc.vector.tensor_tensor(placed[:].indirect(offsets[:, lo // 16:hi // 16]), dp[:, lo:hi], twice_sig[:, lo:hi], ALU.mult)
+        for lo in range(0, SLOTS, HALF):
+            hi = lo + HALF
+            nc.scalar.activation(dp[:, lo:hi], c0[:, lo:hi], ACT.Identity, bias=dz[:], scale=z_inv[:])
+            nc.vector.tensor_tensor(placed[:].indirect(listed(lo, hi)), dp[:, lo:hi], sig[:, lo:hi], ALU.mult)
 
-        for lo, hi in ((0, 256), (256, 768), (768, 1280), (1280, 1792), (1792, POOL)):
+        for lo, hi in zip(STORE_EDGES[:-1], STORE_EDGES[1:]):
             total = sbuf(f"total{lo}", [P, hi - lo], F32)
             nc.vector.tensor_tensor(total[:], placed[:, lo:hi], old_sb[:, lo:hi], ALU.add)
             nc.sync.dma_start(out=out[:, lo:hi], in_=total[:])

from contextlib import ExitStack

import concourse.mybir as mybir

F32 = mybir.dt.float32
BF16 = mybir.dt.bfloat16
I32 = mybir.dt.int32
U32 = mybir.dt.uint32
U16 = mybir.dt.uint16
U8 = mybir.dt.uint8
FP8X4 = mybir.dt.float8_e4m3fn_x4
ALU = mybir.AluOpType
ACT = mybir.ActivationFunctionType
AX = mybir.AxisListType

P = 128
PACK = 4
QUADRANT = 32
SCALE_ROWS = 16
LIST_ROWS = 16
POOL = 2048
SLOTS = 512
ROWS = 128
HIDDEN = 512
PAGE = 16
CHUNK = 128
PAGES = CHUNK // PAGE
HALF = SLOTS // 2
W_SCALAR = 80
STORE_EDGES = (0, 256, 768, 1280, 1792, POOL)

FLOPS = 2 * 512 * SLOTS * (ROWS + HIDDEN + ROWS)


def tile_attend_blrcentred_capped_kernel(tc, query, keys_words, keys_scales, th, reserve, tab_words, tab_scales,
                                          w1, share, gout, hsc, old, offs, out):
    nc = tc.nc
    with ExitStack() as ctx:
        sb = ctx.enter_context(tc.tile_pool(name="sb", bufs=1))
        ps = ctx.enter_context(tc.psum_pool(name="ps", bufs=1))

        def sbuf(name, shape, dtype, tag=None):
            return sb.tile(shape, dtype, name=name, tag=tag or name, align_bytes=64)

        def load_scale_rows(plane, scales):
            for j in range(PACK):
                nc.sync.dma_start(out=plane[j:P:QUADRANT, :].bitcast(I32),
                                  in_=scales[0, j:SCALE_ROWS:PACK, :].bitcast(I32))

        def load_words(pool_words, words):
            nc.sync.dma_start(out=pool_words[:], in_=words[0].rearrange("p n t -> p (n t)").bitcast(I32))

        def listed(lo, hi):
            return offsets[:, lo // LIST_ROWS:hi // LIST_ROWS]

        def interleaved(grouped, raw):
            return grouped[:].rearrange("p (c i) j -> p c j i", i=4), raw[:].rearrange("p j (c i) -> p c j i", i=4)

        def quantize(codes, scales, grouped):
            nc.vector.quantize_mx(out=codes.bitcast(FP8X4), scales=scales, in_=grouped)

        def product(acc, lhs_codes, lhs_scales, rhs_codes, rhs_scales):
            nc.tensor.matmul_mx(out=acc, lhsT=lhs_codes.bitcast(FP8X4), lhsT_scale=lhs_scales,
                                rhs=rhs_codes.bitcast(FP8X4), rhs_scale=rhs_scales, start=True, stop=True)

        offsets = sbuf("offsets", [P, SLOTS // LIST_ROWS], U16)
        tab_plane = sbuf("tab_plane", [P, POOL], U8)
        tab_pool = sbuf("tab_pool", [P, POOL], I32)
        keys_plane = sbuf("keys_plane", [P, POOL], U8)
        keys_pool = sbuf("keys_pool", [P, POOL], I32)
        g_raw = sbuf("g_raw", [P, PACK, ROWS], F32)
        old_sb = sbuf("old_sb", [P, POOL], F32)
        placed = sbuf("placed", [P, POOL], F32)
        w_raw = sbuf("w_raw", [P, PACK, HIDDEN], F32)
        q_raw = sbuf("q_raw", [P, PACK, ROWS], F32)
        share_sb = sbuf("share_sb", [P, PACK], F32)
        hsc_sb = sbuf("hsc_sb", [P, PACK], F32)
        th_sb = sbuf("th_sb", [P, 1], F32)
        reserve_sb = sbuf("reserve_sb", [P, 1], F32)

        nc.vector.memset(tab_plane[:].bitcast(I32), 0)
        nc.vector.memset(keys_plane[:].bitcast(I32), 0)
        nc.vector.memset(placed[:], 0.0)

        nc.sync.dma_start(offsets[:], offs)
        nc.sync.dma_start(out=share_sb[:], in_=share.rearrange("(p t) o -> p (t o)", t=PACK))
        nc.sync.dma_start(out=w_raw[:], in_=w1.rearrange("(p j) c -> p j c", j=PACK))
        load_scale_rows(tab_plane, tab_scales)
        load_words(tab_pool, tab_words)
        nc.sync.dma_start(out=q_raw[:], in_=query.rearrange("(p j) q -> p j q", j=PACK))
        load_words(keys_pool, keys_words)
        load_scale_rows(keys_plane, keys_scales)
        nc.gpsimd.dma_start(out=hsc_sb[:], in_=hsc.rearrange("(p t) o -> p (t o)", t=PACK))
        nc.sync.dma_start(out=th_sb[:], in_=th)
        nc.sync.dma_start(out=g_raw[:], in_=gout.rearrange("(p j) q -> p j q", j=PACK))
        nc.sync.dma_start(out=reserve_sb[:], in_=reserve)
        nc.sync.dma_start(out=old_sb[:], in_=old)

        w_grouped = sbuf("w_grouped", [P, PACK, P, PACK], BF16)
        w_dst = w_grouped[:].rearrange("p t m j -> p m j t")
        w_src = w_raw[:].rearrange("p j (m t) -> p m j t", t=PACK)
        nc.scalar.copy(w_dst[:, 0:W_SCALAR], w_src[:, 0:W_SCALAR])
        nc.vector.tensor_copy(w_dst[:, W_SCALAR:P], w_src[:, W_SCALAR:P])
        tab_scale = sbuf("tab_scale", [P, SLOTS], U8)
        nc.vector.tensor_copy(tab_scale[:], tab_plane[:].indirect(offsets[:]))
        w_codes = sbuf("w_codes", [P, HIDDEN], U32)
        w_scale = sbuf("w_scale", [P, HIDDEN], U8)
        quantize(w_codes[:], w_scale[:], w_grouped[:].rearrange("p t m j -> p (t m j)"))
        tab_codes = sbuf("tab_codes", [P, SLOTS], U32)
        for lo in range(0, SLOTS, HALF):
            nc.vector.tensor_copy(tab_codes[:, lo:lo + HALF], tab_pool[:].bitcast(U32).indirect(listed(lo, lo + HALF)))

        def layer_product(c):
            cols = slice(c * CHUNK, (c + 1) * CHUNK)
            zh = ps.tile([P, PACK, CHUNK], F32, name=f"zh{c}")
            for t in range(PACK):
                feats = slice(t * P, (t + 1) * P)
                product(zh[:, t, :], w_codes[:, feats], w_scale[:, feats], tab_codes[:, cols], tab_scale[:, cols])
            return zh

        def page_sums(sums, zh):
            nc.vector.tensor_reduce(sums, zh[:].rearrange("p t (g j) -> p g t j", j=PAGE), AX.X, ALU.add)

        def page_shift(shift, sums, pages):
            nc.vector.scalar_tensor_tensor(shift, sums, 1.0 / PAGE,
                                           share_sb[:].unsqueeze(1).to_broadcast([P, pages, PACK]), ALU.mult, ALU.mult)

        def centre_interleaved(centred, zh, shift):
            nc.vector.tensor_tensor(centred[:], zh[:].rearrange("p t (g j) -> p g j t", j=PAGE),
                                    shift.unsqueeze(2).to_broadcast([P, PAGES, PAGE, PACK]), ALU.subtract)

        def scale_hidden(hs, hv, slots):
            nc.vector.tensor_tensor(hs[:], hv[:], hsc_sb[:].unsqueeze(1).to_broadcast([P, slots, PACK]), ALU.mult)

        zh0 = layer_product(0)
        sums0 = sbuf("sums0", [P, PAGES, PACK], F32)
        page_sums(sums0[:], zh0)
        shift0 = sbuf("shift0", [P, PAGES, PACK], F32)
        page_shift(shift0[:], sums0[:], PAGES)
        centred0 = sbuf("centred0", [P, PACK, PAGES, PAGE], F32)
        nc.vector.tensor_tensor(centred0[:], zh0[:].rearrange("p t (g j) -> p t g j", j=PAGE),
                                shift0[:].rearrange("p g t -> p t g").unsqueeze(3).to_broadcast([P, PACK, PAGES, PAGE]),
                                ALU.subtract)
        hv0 = sbuf("hv0", [P, PACK, CHUNK], F32)
        nc.scalar.activation(hv0[:].rearrange("p t i -> p (t i)"), centred0[:].rearrange("p t g j -> p (t g j)"), ACT.Tanh)
        hs0 = sbuf("hs0", [P, CHUNK, PACK], BF16)
        for t in range(PACK):
            nc.scalar.activation(hs0[:, :, t], hv0[:, t, :], ACT.Copy, scale=hsc_sb[:, t:t + 1])

        zh1 = layer_product(1)
        sums1 = sbuf("sums1", [P, PAGES, PACK], F32)
        page_sums(sums1[:], zh1)
        shift1 = sbuf("shift1", [P, PAGES, PACK], F32)
        page_shift(shift1[:], sums1[:], PAGES)
        centred1 = sbuf("centred1", [P, PAGES, PAGE, PACK], F32)
        centre_interleaved(centred1, zh1, shift1[:])
        hv1 = sbuf("hv1", [P, CHUNK, PACK], F32)
        nc.scalar.activation(hv1[:].rearrange("p i t -> p (i t)"), centred1[:].rearrange("p g j t -> p (g j t)"), ACT.Tanh)
        g_grouped = sbuf("g_grouped", [P, ROWS, PACK], BF16, tag="centred1")
        nc.scalar.copy(*interleaved(g_grouped, g_raw))

        q_grouped = sbuf("q_grouped", [P, ROWS, PACK], BF16)
        nc.scalar.copy(*interleaved(q_grouped, q_raw))
        q_codes = sbuf("q_codes", [P, ROWS], U32)
        q_scale = sbuf("q_scale", [P, ROWS], U8)
        quantize(q_codes[:], q_scale[:], q_grouped[:].rearrange("p q j -> p (q j)"))
        keys_codes = sbuf("keys_codes", [P, SLOTS], U32)
        nc.vector.tensor_copy(keys_codes[:], keys_pool[:].bitcast(U32).indirect(offsets[:]))
        keys_scale = sbuf("keys_scale", [P, SLOTS], U8, tag="keys_pool")
        nc.vector.tensor_copy(keys_scale[:], keys_plane[:].indirect(offsets[:]))
        score = ps.tile([P, SLOTS], F32, name="score")
        product(score[:], q_codes[:], q_scale[:], keys_codes[:], keys_scale[:])
        half_th = sbuf("half_th", [P, 1], F32, tag="shift1")
        nc.scalar.activation(half_th[:], th_sb[:], ACT.Copy, scale=-0.5)
        tanh_half = sbuf("tanh_half", [P, SLOTS], F32)
        nc.scalar.activation(tanh_half[:], score[:], ACT.Tanh, bias=half_th[:], scale=0.5)
        tanh_abs = sbuf("tanh_abs", [P, SLOTS], F32)
        nc.scalar.activation(tanh_abs[:], tanh_half[:], ACT.Abs)

        late_sums = sbuf("late_sums", [P, 2 * PAGES, PACK], F32, tag="keys_plane")
        late_shift = sbuf("late_shift", [P, 2 * PAGES, PACK], F32)
        late_hv = sbuf("late_hv", [P, HALF, PACK], F32)
        late_zh = [layer_product(c) for c in range(HALF // CHUNK, SLOTS // CHUNK)]
        for k in range(HALF // CHUNK):
            page_sums(late_sums[:, k * PAGES:(k + 1) * PAGES], late_zh[k])
        page_shift(late_shift[:], late_sums[:], 2 * PAGES)
        for k in range(HALF // CHUNK):
            centred = sbuf(f"centred{HALF // CHUNK + k}", [P, PAGES, PAGE, PACK], F32)
            centre_interleaved(centred, late_zh[k], late_shift[:, k * PAGES:(k + 1) * PAGES])
            nc.scalar.activation(late_hv[:, k * CHUNK:(k + 1) * CHUNK].rearrange("p i t -> p (i t)"),
                                 centred[:].rearrange("p g j t -> p (g j t)"), ACT.Tanh)

        log_sig = sbuf("log_sig", [P, SLOTS], F32, tag="centred3")
        log_sum = sbuf("log_sum", [P, 1], F32)
        nc.scalar.activation(log_sig[:], tanh_abs[:], ACT.Ln, bias=0.5, scale=0.5, accum_out=log_sum[:])
        relu_half = sbuf("relu_half", [P, SLOTS], F32, tag="tanh_abs")
        relu_sum = sbuf("relu_sum", [P, 1], F32)
        nc.scalar.activation(relu_half[:], score[:], ACT.Relu, bias=half_th[:], scale=0.5, accum_out=relu_sum[:])
        z_part = sbuf("z_part", [P, 1], F32)
        nc.scalar.activation(z_part[:], log_sum[:], ACT.Identity, bias=reserve_sb[:], scale=-1.0)
        z = sbuf("z", [P, 1], F32)
        nc.scalar.activation(z[:], relu_sum[:], ACT.Identity, bias=z_part[:], scale=2.0)
        sig = sbuf("sig", [P, SLOTS], F32, tag="log_sum")
        nc.scalar.activation(sig[:], tanh_half[:], ACT.Identity, bias=256.0, scale=256.0)

        c0 = ps.tile([P, SLOTS], F32, name="c0")
        g_codes = sbuf("g_codes", [P, ROWS], U32, tag="keys_pool")
        g_scale = sbuf("g_scale", [P, ROWS], U8)
        quantize(g_codes[:], g_scale[:], g_grouped[:].rearrange("p q j -> p (q j)"))

        def read_product(name, hs, lo, hi, tag=None):
            codes = sbuf(name + "_codes", [P, hi - lo], U32, tag=tag)
            scales = sbuf(name + "_scale", [P, hi - lo], U8)
            quantize(codes[:], scales[:], hs[:].rearrange("p i t -> p (i t)"))
            product(c0[:, lo:hi], g_codes[:], g_scale[:], codes[:], scales[:])

        hs1 = sbuf("hs1", [P, CHUNK, PACK], BF16, tag="late_shift")
        scale_hidden(hs1, hv1, CHUNK)
        read_product("hs0", hs0, 0, CHUNK, tag="keys_plane")
        late_hs = sbuf("late_hs", [P, HALF, PACK], BF16)
        scale_hidden(late_hs, late_hv, HALF)
        read_product("hs1", hs1, CHUNK, HALF)
        read_product("late_hs", late_hs, HALF, SLOTS)

        log_terms = sbuf("log_terms", [P, SLOTS], F32)
        log_dot = sbuf("log_dot", [P, 1], F32)
        nc.vector.scalar_tensor_tensor(log_terms[:], c0[:], 1.0, log_sig[:], ALU.mult, ALU.mult, accum_out=log_dot[:])
        relu_terms = sbuf("relu_terms", [P, SLOTS], F32)
        relu_dot = sbuf("relu_dot", [P, 1], F32)
        nc.vector.scalar_tensor_tensor(relu_terms[:], c0[:], -2.0, relu_half[:], ALU.mult, ALU.mult, accum_out=relu_dot[:])
        z_inv = sbuf("z_inv", [P, 1], F32)
        nc.vector.reciprocal(z_inv[:], z[:])
        dz_z = sbuf("dz_z", [P, 1], F32)
        nc.vector.tensor_scalar(dz_z[:], log_dot[:], relu_dot[:], z_inv[:], ALU.add, ALU.mult)
        dz = sbuf("dz", [P, 1], F32)
        nc.scalar.activation(dz[:], dz_z[:], ACT.Copy, scale=z_inv[:])

        dp = sbuf("dp", [P, SLOTS], F32)
        for lo in range(0, SLOTS, HALF):
            hi = lo + HALF
            nc.scalar.activation(dp[:, lo:hi], c0[:, lo:hi], ACT.Identity, bias=dz[:], scale=z_inv[:])
            nc.vector.tensor_tensor(placed[:].indirect(listed(lo, hi)), dp[:, lo:hi], sig[:, lo:hi], ALU.mult)

        for lo, hi in zip(STORE_EDGES[:-1], STORE_EDGES[1:]):
            total = sbuf(f"total{lo}", [P, hi - lo], F32)
            nc.vector.tensor_tensor(total[:], placed[:, lo:hi], old_sb[:, lo:hi], ALU.add)
            nc.sync.dma_start(out=out[:, lo:hi], in_=total[:])
